import numpy as np, ml_dtypes
CORES = [22,46,70,150,174,198,278,302,326,406,430,454]
N = 12
import mx_ref
NC, KB = 128, 1
BF = ml_dtypes.bfloat16
def cut(t, i, w=512):
    return t[:, w * i:w * i + w]
def term(a, B):
    return np.stack([mx_ref.matmul(mx_ref.quantize(cut(a, i)), B) for i in range(4)], axis=2).reshape(128, -1)
def setup_inputs(rng):
    def f(*shape):
        return mx_ref.flush((rng.standard_normal(shape, dtype=np.float32) * np.exp2(rng.integers(-2, 3, shape[:-1] + (1,)))).astype(BF))
    return {"a": f(N, 128, 4 * 512), "b": f(N, 128, KB * 4 * NC)}
def setup_inputs_blocks(rng):
    d = setup_inputs(rng)
    for k in ("a", "b"): d[k] = mx_ref.spread(d[k], rng, 2)
    return d
def setup_inputs_wide(rng):
    d = setup_inputs(rng)
    for k in ("a", "b"): d[k] = mx_ref.flush((d[k].astype(np.float32) * np.exp2(rng.integers(-4, 5, (N, 1, 1))).astype(np.float32)).astype(BF))
    return d
def setup_inputs_lossless(rng):
    a = np.zeros((N, 128, 4 * 128, 4), np.float32)
    for r in range(N):
        k = rng.integers(0, 512, size=4 * 128)
        a[r, k // 4, np.arange(4 * 128), k % 4] = 1.0
    size = np.repeat(2.0 ** rng.integers(-4, 5, size=(1, 1, (KB * 4 * NC) // 4)), 4, axis=2)
    b = rng.integers(-1, 2, size=(N, 128, KB * 4 * NC)) * size
    return {"a": a.reshape(N, 128, 4 * 512).astype(BF), "b": b.astype(np.float32).astype(BF)}
def reference(a, b):
    y = np.zeros((N, 128, KB * 4 * NC), np.float32)
    for k in range(KB):
        y[:, :, 4 * NC * k:4 * NC * k + 4 * NC] = mx_ref.total([term(a[r], mx_ref.quantize(cut(b[r], k, 4 * NC))) for r in range(N)])
    return {"y": y}

@@ -1,0 +1,193 @@
+from concourse.bass import DstId, RemoteDMATransfer
+from concourse.mybir import dt, AluOpType, ActivationFunctionType
+
+NCOL = 128
+W = [48, 32, 48]
+C0 = [0, 48, 80]
+WIN = 64
+WIN0 = [0, 32, 64]
+WMAX = 48
+
+CODE, U8, BF, F32 = "float8_e4m3fn_x4", "uint8", "bfloat16", "float32"
+SCRATCH = {
+    "ta": ("sbuf", [128, 2048], BF), "tb": ("sbuf", [128, 512], BF),
+    "ones": ("sbuf", [128, 128], BF), "ident": ("sbuf", [128, 128], BF), "tz": ("sbuf", [128, 2048], BF),
+    "tt": ("sbuf", [128, 512], BF), "st": ("sbuf", [128, 512], BF), "et": ("sbuf", [128, 512], BF),
+    "tmp": ("sbuf", [128, 4 * WMAX], F32), "tmp2": ("sbuf", [128, 4 * WMAX], F32),
+    "ysb": ("sbuf", [128, 512], F32),
+    "qa": ("sbuf", [128, 512], CODE), "qa_s": ("sbuf", [128, 512], U8),
+    "qb": ("sbuf", [128, 128], CODE), "qb_s": ("sbuf", [128, 128], U8),
+    "qz": ("sbuf", [128, 512], CODE), "qz_s": ("sbuf", [128, 512], U8),
+    "qt": ("sbuf", [128, 128], CODE), "qt_s": ("sbuf", [128, 128], U8),
+    "qs": ("sbuf", [128, 128], CODE), "qs_s": ("sbuf", [128, 128], U8),
+    "L": ("sbuf", [128, 2 * WMAX + 2 * WIN], CODE), "L_s": ("sbuf", [128, 2 * WMAX + 2 * WIN], U8),
+    "F": ("sbuf", [128, 3 * NCOL], CODE), "F_s": ("sbuf", [128, 3 * NCOL], U8),
+    "ps": ("psum", [128, 512 * 8], F32),
+}
+SEMAPHORES = ["ld_b", "ld_a0", "ld_a1", "ld_a2", "ld_a3", "c_one", "c_mem", "c_id", "c_z", "c_qz", "q_b", "q_a", "p_t",
+              "cp_t", "q_t", "u1", "v1", "q_s", "u2", "v2", "q_e", "fin", "ycp", "sty",
+              "arrA", "arrNm", "arrNp", "arrD", "arrE", "arrDp", "left"]
+
+
+def rank_program(g, core, T, topo):
+    if T.rank_of(core) is None:
+        return
+    S = T.sem
+    hosts = sorted({topo.host(c) for c in T.cores})
+    lanes = {h: [c for c in T.cores if topo.host(c) == h] for h in hosts}
+    ring = [hosts[0]]
+    while len(ring) < len(hosts):
+        ring.append([x for x in hosts if x not in ring and topo.may_write(lanes[ring[-1]][0], lanes[x][0])][0])
+    h = topo.host(core)
+    l = lanes[h].index(core)
+    pos = ring.index(h)
+    nxt = lanes[ring[(pos + 1) % len(ring)]][l]
+    prv = lanes[ring[(pos - 1) % len(ring)]][l]
+    peers = [(l + 1) % 3, (l + 2) % 3]
+    w, c0 = W[l], C0[l]
+
+    def xoff(p, lane):
+        order = [(p + 1) % 3, (p + 2) % 3, p]
+        return sum(W[q] for q in order[:order.index(lane)])
+
+    def bits(dsts):
+        m = topo.mask(core, dsts[0])
+        for d in dsts[1:]:
+            m &= topo.mask(core, d)
+        return [1 << i for i in range(16) if (m >> i) & 1]
+
+    def did(d):
+        rid, pid = topo.addr(d, core)
+        return DstId(rid=rid, pnc=pid)
+
+    def send(pairs, sem):
+        eng = bits([p[0] for p in pairs])
+        k = len(eng) // len(pairs)
+        for plane in (False, True):
+            tr = []
+            for i, (d, sb, a, b, lb, c) in enumerate(pairs):
+                if plane:
+                    src, dst = T[sb + "_s"][:, a:b], T[lb + "_s"][:, c:c + b - a]
+                else:
+                    src, dst = T[sb][:, a:b].bitcast(dt.uint8), T[lb][:, c:c + b - a].bitcast(dt.uint8)
+                tr.append(RemoteDMATransfer(dst_ids=[did(d)], dma_engine_mask=sum(eng[i * k:(i + 1) * k]),
+                                            remote_sem=sem, src=src, dst=dst))
+            g.remote_dma_fused(tr, local_sem=S.left)
+        return 2 * k * len(pairs)
+
+    V, SC, TE, SY = g.vector, g.scalar, g.tensor, g.sync
+    bank = lambda i, a, b: T.ps[:, 512 * i + a:512 * i + b]
+    ld_a = [S.ld_a0, S.ld_a1, S.ld_a2, S.ld_a3]
+
+    SY.dma_start(T.tb[:], T.b[:]).then_inc(S.ld_b, 16)
+    for t in range(4):
+        (SC if t % 2 == 0 else SY).dma_start(T.ta[:, 512 * t:512 * t + 512], T.a[:, 512 * t:512 * t + 512]).then_inc(ld_a[t], 16)
+
+    V.memset(T.ones[:], 1.0).then_inc(S.c_one, 1)
+    V.memset(T.tz[:], 0.0).then_inc(S.c_mem, 1)
+    V.memset(T.st[:], 0.0).then_inc(S.c_mem, 1)
+    V.memset(T.et[:], 0.0).then_inc(S.c_mem, 1)
+    g.wait_ge(S.c_one, 1)
+    g.affine_select(T.ident[:], T.ones[:], [[-1, 128]], AluOpType.is_equal, 0.0, 0, 1).then_inc(S.c_id, 1)
+    V.wait_ge(S.c_mem, 3)
+    V.wait_ge(S.c_id, 1)
+    for t in range(4):
+        V.tensor_copy(T.tz[:, 512 * t + t:512 * t + 512:4], T.ident[:]).then_inc(S.c_z, 1)
+    V.wait_ge(S.c_z, 4)
+    V.quantize_mx(T.qz[:], T.qz_s[:], T.tz[:]).then_inc(S.c_qz, 1)
+
+    V.wait_ge(S.ld_b, 16)
+    V.quantize_mx(T.qb[:], T.qb_s[:], T.tb[:]).then_inc(S.q_b, 1)
+    TE.wait_ge(S.q_b, 1)
+    for t in range(4):
+        cs = slice(128 * t, 128 * t + 128)
+        V.wait_ge(ld_a[t], 16)
+        V.quantize_mx(T.qa[:, cs], T.qa_s[:, cs], T.ta[:, 512 * t:512 * t + 512]).then_inc(S.q_a, 1)
+        TE.wait_ge(S.q_a, t + 1)
+        TE.matmul_mx(bank(t, 0, 128), T.qa[:, cs], T.qa_s[:, cs], T.qb[:], T.qb_s[:], True, True).then_inc(S.p_t, 1)
+        if t < 3:
+            SC.wait_ge(S.p_t, t + 1)
+            SC.activation(T.tt[:, t:512:4], bank(t, 0, 128), ActivationFunctionType.Copy).then_inc(S.cp_t, 1)
+    V.wait_ge(S.p_t, 4)
+    V.tensor_copy(T.tt[:, 3:512:4], bank(3, 0, 128)).then_inc(S.cp_t, 1)
+    V.wait_ge(S.cp_t, 4)
+    V.quantize_mx(T.qt[:], T.qt_s[:], T.tt[:]).then_inc(S.q_t, 1)
+
+    left = 0
+    g.wait_ge(S.q_t, 1)
+    left += send([(lanes[h][p], "qt", WIN0[p], WIN0[p] + WIN, "L", 2 * W[p] + WIN * (0 if l == (p + 1) % 3 else 1))
+                  for p in peers], S.arrA)
+
+    def sel(t):
+        return T.qz[:, 128 * t:128 * t + 128], T.qz_s[:, 128 * t:128 * t + 128]
+
+    def unpack(first_bank, buf, col, start, stop, sem):
+        for t in range(4):
+            z, zs = sel(t)
+            i = TE.matmul_mx(bank(first_bank + t, 0, 128), z, zs, T[buf][:, col:col + 128], T[buf + "_s"][:, col:col + 128],
+                             start, stop)
+            if sem is not None:
+                i.then_inc(sem, 1)
+
+    def add3(first_bank, o1, o2, own, ostart, tmp, out, usem, vsem):
+        for t in range(4):
+            V.wait_ge(usem, t + 1)
+            V.tensor_tensor(tmp[:, WMAX * t:WMAX * t + w], bank(first_bank + t, o1, o1 + w),
+                            own[:, 4 * ostart + t:4 * (ostart + w):4], AluOpType.add).then_inc(vsem, 1)
+            V.wait_ge(vsem, 2 * t + 1)
+            V.tensor_tensor(out[:, t:4 * w:4], bank(first_bank + t, o2, o2 + w), tmp[:, WMAX * t:WMAX * t + w],
+                            AluOpType.add).then_inc(vsem, 1)
+        V.wait_ge(vsem, 8)
+
+    off = c0 - WIN0[l]
+    TE.wait_ge(S.c_qz, 1)
+    TE.wait_ge(S.arrA, 16)
+    unpack(4, "L", 2 * w, True, True, S.u1)
+    add3(4, off, WIN + off, T.tt, c0, T.tmp, T.st, S.u1, S.v1)
+    V.quantize_mx(T.qs[:], T.qs_s[:], T.st[:]).then_inc(S.q_s, 1)
+
+    g.wait_ge(S.q_s, 1)
+    left += send([(prv, "qs", 0, w, "L", w)], S.arrNp)
+    left += send([(nxt, "qs", 0, w, "L", 0)], S.arrNm)
+    g.wait_ge(S.arrNp, 16)
+    left += send([(prv, "L", w, 2 * w, "F", xoff(l, l))], S.arrD)
+
+    TE.wait_ge(S.arrNp, 16)
+    TE.wait_ge(S.arrNm, 16)
+    TE.wait_ge(S.cp_t, 4)
+    unpack(0, "L", 0, True, True, S.u2)
+    add3(0, 0, w, T.st, 0, T.tmp2, T.et, S.u2, S.v2)
+    e0 = NCOL + xoff(l, l)
+    V.quantize_mx(T.F[:, e0:e0 + 128], T.F_s[:, e0:e0 + 128], T.et[:]).then_inc(S.q_e, 1)
+    g.wait_ge(S.q_e, 1)
+    left += send([(lanes[h][p], "F", e0, e0 + w, "F", NCOL + xoff(p, l)) for p in peers], S.arrE)
+
+    g.wait_ge(S.arrD, 16)
+    left += send([(lanes[h][p], "F", xoff(l, l), xoff(l, l) + w, "F", xoff(p, l)) for p in peers], S.arrDp)
+
+    TE.wait_ge(S.arrE, 16)
+    TE.wait_ge(S.q_e, 1)
+    TE.wait_ge(S.v1, 8)
+    unpack(4, "F", NCOL, True, False, None)
+    TE.wait_ge(S.arrD, 16)
+    TE.wait_ge(S.arrDp, 16)
+    unpack(4, "F", 0, False, True, S.fin)
+    segs = []
+    for q in peers + [l]:
+        if segs and segs[-1][1] + segs[-1][2] == C0[q]:
+            segs[-1] = (segs[-1][0], segs[-1][1], segs[-1][2] + W[q])
+        else:
+            segs.append((xoff(l, q), C0[q], W[q]))
+    for t in range(4):
+        E = V if t % 2 == 0 else SC
+        E.wait_ge(S.fin, t + 1)
+        for x, j, n in segs:
+            if t % 2 == 0:
+                V.tensor_copy(T.ysb[:, 4 * j + t:4 * (j + n):4], bank(4 + t, x, x + n)).then_inc(S.ycp, 1)
+            else:
+                SC.activation(T.ysb[:, 4 * j + t:4 * (j + n):4], bank(4 + t, x, x + n),
+                              ActivationFunctionType.Copy).then_inc(S.ycp, 1)
+    SY.wait_ge(S.ycp, 4 * len(segs))
+    SY.dma_start(T.y[:], T.ysb[:]).then_inc(S.sty, 16)
+    SY.wait_ge(S.sty, 16)
+    g.wait_ge(S.left, left)

@@ -4,8 +4,6 @@ from concourse.mybir import dt, AluOpType, ActivationFunctionType
 NCOL = 128
 W = [48, 32, 48]
 C0 = [0, 48, 80]
-WIN = 64
-WIN0 = [0, 32, 64]
 WMAX = 48
 
 CODE, U8, BF, F32 = "float8_e4m3fn_x4", "uint8", "bfloat16", "float32"
@@ -13,20 +11,19 @@ SCRATCH = {
     "ta": ("sbuf", [128, 2048], BF), "tb": ("sbuf", [128, 512], BF),
     "ones": ("sbuf", [128, 128], BF), "ident": ("sbuf", [128, 128], BF), "tz": ("sbuf", [128, 2048], BF),
     "tt": ("sbuf", [128, 512], BF), "st": ("sbuf", [128, 512], BF), "et": ("sbuf", [128, 512], BF),
-    "tmp": ("sbuf", [128, 4 * WMAX], F32), "tmp2": ("sbuf", [128, 4 * WMAX], F32),
+    "tmp": ("sbuf", [128, 4 * WMAX], F32), "tmp2": ("sbuf", [128, 4 * WMAX], F32), "es": ("sbuf", [128, 4 * WMAX], F32),
     "ysb": ("sbuf", [128, 512], F32),
     "qa": ("sbuf", [128, 512], CODE), "qa_s": ("sbuf", [128, 512], U8),
     "qb": ("sbuf", [128, 128], CODE), "qb_s": ("sbuf", [128, 128], U8),
     "qz": ("sbuf", [128, 512], CODE), "qz_s": ("sbuf", [128, 512], U8),
-    "qt": ("sbuf", [128, 128], CODE), "qt_s": ("sbuf", [128, 128], U8),
-    "qs": ("sbuf", [128, 128], CODE), "qs_s": ("sbuf", [128, 128], U8),
-    "L": ("sbuf", [128, 2 * WMAX + 2 * WIN], CODE), "L_s": ("sbuf", [128, 2 * WMAX + 2 * WIN], U8),
-    "F": ("sbuf", [128, 3 * NCOL], CODE), "F_s": ("sbuf", [128, 3 * NCOL], U8),
+    "L": ("sbuf", [128, 4 * WMAX + NCOL], CODE), "L_s": ("sbuf", [128, 4 * WMAX + NCOL], U8),
+    "G": ("sbuf", [128, NCOL + WMAX], CODE), "G_s": ("sbuf", [128, NCOL + WMAX], U8),
+    "F": ("sbuf", [128, 2 * NCOL], CODE), "F_s": ("sbuf", [128, 2 * NCOL], U8),
     "ps": ("psum", [128, 512 * 8], F32),
 }
-SEMAPHORES = ["ld_b", "ld_a0", "ld_a1", "ld_a2", "ld_a3", "c_one", "c_mem", "c_id", "c_z", "c_qz", "q_b", "q_a", "p_t",
-              "cp_t", "q_t", "u1", "v1", "q_s", "u2", "v2", "q_e", "fin", "ycp", "sty",
-              "arrA", "arrNm", "arrNp", "arrD", "arrE", "arrDp", "left"]
+SEMAPHORES = ["ld_b", "ld_a0", "ld_a3", "c_one", "c_mem", "c_id", "c_z", "c_qz", "q_b", "q_a", "p_t",
+              "cp_t", "q_t", "u1", "v1", "q_s", "u2", "v2", "u3", "v3", "q_e", "fin", "ycp", "sty",
+              "arrA", "arrNm", "arrNp", "arrD", "arrE", "left"]
 
 
 def rank_program(g, core, T, topo):
@@ -45,6 +42,7 @@ def rank_program(g, core, T, topo):
     prv = lanes[ring[(pos - 1) % len(ring)]][l]
     peers = [(l + 1) % 3, (l + 2) % 3]
     w, c0 = W[l], C0[l]
+    q0 = 2 * w + 2 * WMAX
 
     def xoff(p, lane):
         order = [(p + 1) % 3, (p + 2) % 3, p]
@@ -77,31 +75,28 @@ def rank_program(g, core, T, topo):
 
     V, SC, TE, SY = g.vector, g.scalar, g.tensor, g.sync
     bank = lambda i, a, b: T.ps[:, 512 * i + a:512 * i + b]
-    ld_a = [S.ld_a0, S.ld_a1, S.ld_a2, S.ld_a3]
 
     SY.dma_start(T.tb[:], T.b[:]).then_inc(S.ld_b, 16)
-    for t in range(4):
-        (SC if t % 2 == 0 else SY).dma_start(T.ta[:, 512 * t:512 * t + 512], T.a[:, 512 * t:512 * t + 512]).then_inc(ld_a[t], 16)
+    SC.dma_start(T.ta[:, 0:1536], T.a[:, 0:1536]).then_inc(S.ld_a0, 16)
+    SY.dma_start(T.ta[:, 1536:2048], T.a[:, 1536:2048]).then_inc(S.ld_a3, 16)
 
     V.memset(T.ones[:], 1.0).then_inc(S.c_one, 1)
     V.memset(T.tz[:], 0.0).then_inc(S.c_mem, 1)
-    V.memset(T.st[:], 0.0).then_inc(S.c_mem, 1)
-    V.memset(T.et[:], 0.0).then_inc(S.c_mem, 1)
     g.wait_ge(S.c_one, 1)
     g.affine_select(T.ident[:], T.ones[:], [[-1, 128]], AluOpType.is_equal, 0.0, 0, 1).then_inc(S.c_id, 1)
-    V.wait_ge(S.c_mem, 3)
+    V.wait_ge(S.c_mem, 1)
     V.wait_ge(S.c_id, 1)
     for t in range(4):
         V.tensor_copy(T.tz[:, 512 * t + t:512 * t + 512:4], T.ident[:]).then_inc(S.c_z, 1)
-    V.wait_ge(S.c_z, 4)
-    V.quantize_mx(T.qz[:], T.qz_s[:], T.tz[:]).then_inc(S.c_qz, 1)
 
     V.wait_ge(S.ld_b, 16)
     V.quantize_mx(T.qb[:], T.qb_s[:], T.tb[:]).then_inc(S.q_b, 1)
     TE.wait_ge(S.q_b, 1)
+    V.wait_ge(S.ld_a0, 16)
     for t in range(4):
         cs = slice(128 * t, 128 * t + 128)
-        V.wait_ge(ld_a[t], 16)
+        if t == 3:
+            V.wait_ge(S.ld_a3, 16)
         V.quantize_mx(T.qa[:, cs], T.qa_s[:, cs], T.ta[:, 512 * t:512 * t + 512]).then_inc(S.q_a, 1)
         TE.wait_ge(S.q_a, t + 1)
         TE.matmul_mx(bank(t, 0, 128), T.qa[:, cs], T.qa_s[:, cs], T.qb[:], T.qb_s[:], True, True).then_inc(S.p_t, 1)
@@ -111,67 +106,71 @@ def rank_program(g, core, T, topo):
     V.wait_ge(S.p_t, 4)
     V.tensor_copy(T.tt[:, 3:512:4], bank(3, 0, 128)).then_inc(S.cp_t, 1)
     V.wait_ge(S.cp_t, 4)
-    V.quantize_mx(T.qt[:], T.qt_s[:], T.tt[:]).then_inc(S.q_t, 1)
+    V.quantize_mx(T.L[:, q0:q0 + 128], T.L_s[:, q0:q0 + 128], T.tt[:]).then_inc(S.q_t, 1)
+    V.wait_ge(S.c_z, 4)
+    V.quantize_mx(T.qz[:], T.qz_s[:], T.tz[:]).then_inc(S.c_qz, 1)
+    V.memset(T.st[:], 0.0).then_inc(S.c_mem, 1)
+    V.memset(T.et[:], 0.0).then_inc(S.c_mem, 1)
+    V.wait_ge(S.c_mem, 3)
 
     left = 0
     g.wait_ge(S.q_t, 1)
-    left += send([(lanes[h][p], "qt", WIN0[p], WIN0[p] + WIN, "L", 2 * W[p] + WIN * (0 if l == (p + 1) % 3 else 1))
-                  for p in peers], S.arrA)
+    left += send([(lanes[h][p], "L", q0 + C0[p], q0 + C0[p] + WMAX, "L",
+                   2 * W[p] + WMAX * (0 if l == (p + 1) % 3 else 1)) for p in peers], S.arrA)
 
-    def sel(t):
-        return T.qz[:, 128 * t:128 * t + 128], T.qz_s[:, 128 * t:128 * t + 128]
-
-    def unpack(first_bank, buf, col, start, stop, sem):
+    def unpack(first_bank, buf, col, sem):
         for t in range(4):
-            z, zs = sel(t)
-            i = TE.matmul_mx(bank(first_bank + t, 0, 128), z, zs, T[buf][:, col:col + 128], T[buf + "_s"][:, col:col + 128],
-                             start, stop)
-            if sem is not None:
-                i.then_inc(sem, 1)
+            TE.matmul_mx(bank(first_bank + t, 0, 128), T.qz[:, 128 * t:128 * t + 128], T.qz_s[:, 128 * t:128 * t + 128],
+                         T[buf][:, col:col + 128], T[buf + "_s"][:, col:col + 128], True, True).then_inc(sem, 1)
 
-    def add3(first_bank, o1, o2, own, ostart, tmp, out, usem, vsem):
+    def add3(first_bank, o1, o2, own, ostart, tmp, outs, usem, vsem):
         for t in range(4):
             V.wait_ge(usem, t + 1)
             V.tensor_tensor(tmp[:, WMAX * t:WMAX * t + w], bank(first_bank + t, o1, o1 + w),
                             own[:, 4 * ostart + t:4 * (ostart + w):4], AluOpType.add).then_inc(vsem, 1)
             V.wait_ge(vsem, 2 * t + 1)
-            V.tensor_tensor(out[:, t:4 * w:4], bank(first_bank + t, o2, o2 + w), tmp[:, WMAX * t:WMAX * t + w],
+            V.tensor_tensor(outs[t], bank(first_bank + t, o2, o2 + w), tmp[:, WMAX * t:WMAX * t + w],
                             AluOpType.add).then_inc(vsem, 1)
         V.wait_ge(vsem, 8)
 
-    off = c0 - WIN0[l]
     TE.wait_ge(S.c_qz, 1)
+    TE.wait_ge(S.q_t, 1)
     TE.wait_ge(S.arrA, 16)
-    unpack(4, "L", 2 * w, True, True, S.u1)
-    add3(4, off, WIN + off, T.tt, c0, T.tmp, T.st, S.u1, S.v1)
-    V.quantize_mx(T.qs[:], T.qs_s[:], T.st[:]).then_inc(S.q_s, 1)
+    unpack(4, "L", 2 * w, S.u1)
+    add3(4, 0, WMAX, T.tt, c0, T.tmp, [T.st[:, t:4 * w:4] for t in range(4)], S.u1, S.v1)
+    V.quantize_mx(T.G[:, 0:128], T.G_s[:, 0:128], T.st[:]).then_inc(S.q_s, 1)
 
     g.wait_ge(S.q_s, 1)
-    left += send([(prv, "qs", 0, w, "L", w)], S.arrNp)
-    left += send([(nxt, "qs", 0, w, "L", 0)], S.arrNm)
+    left += send([(prv, "G", 0, w, "L", w)], S.arrNp)
+    left += send([(nxt, "G", 0, w, "L", 0)], S.arrNm)
     g.wait_ge(S.arrNp, 16)
-    left += send([(prv, "L", w, 2 * w, "F", xoff(l, l))], S.arrD)
+    left += send([(prv, "L", w, 2 * w, "G", NCOL)], S.arrD)
 
     TE.wait_ge(S.arrNp, 16)
     TE.wait_ge(S.arrNm, 16)
     TE.wait_ge(S.cp_t, 4)
-    unpack(0, "L", 0, True, True, S.u2)
-    add3(0, 0, w, T.st, 0, T.tmp2, T.et, S.u2, S.v2)
-    e0 = NCOL + xoff(l, l)
-    V.quantize_mx(T.F[:, e0:e0 + 128], T.F_s[:, e0:e0 + 128], T.et[:]).then_inc(S.q_e, 1)
-    g.wait_ge(S.q_e, 1)
-    left += send([(lanes[h][p], "F", e0, e0 + w, "F", NCOL + xoff(p, l)) for p in peers], S.arrE)
+    unpack(0, "L", 0, S.u2)
+    add3(0, 0, w, T.st, 0, T.tmp2, [T.es[:, WMAX * t:WMAX * t + w] for t in range(4)], S.u2, S.v2)
 
-    g.wait_ge(S.arrD, 16)
-    left += send([(lanes[h][p], "F", xoff(l, l), xoff(l, l) + w, "F", xoff(p, l)) for p in peers], S.arrDp)
+    TE.wait_ge(S.arrD, 16)
+    TE.wait_ge(S.q_s, 1)
+    TE.wait_ge(S.v1, 8)
+    unpack(4, "G", w, S.u3)
+    for t in range(4):
+        V.wait_ge(S.u3, t + 1)
+        V.tensor_tensor(T.et[:, t:4 * w:4], bank(4 + t, NCOL - w, NCOL), T.es[:, WMAX * t:WMAX * t + w],
+                        AluOpType.add).then_inc(S.v3, 1)
+    V.wait_ge(S.v3, 4)
+    e0 = xoff(l, l)
+    V.quantize_mx(T.F[:, e0:e0 + 128], T.F_s[:, e0:e0 + 128], T.et[:]).then_inc(S.q_e, 1)
+
+    g.wait_ge(S.q_e, 1)
+    left += send([(lanes[h][p], "F", e0, e0 + w, "F", xoff(p, l)) for p in peers], S.arrE)
 
     TE.wait_ge(S.arrE, 16)
     TE.wait_ge(S.q_e, 1)
-    TE.wait_ge(S.v1, 8)
-    unpack(4, "F", NCOL, True, False, None)
-    TE.wait_ge(S.arrD, 16)
-    TE.wait_ge(S.arrDp, 16)
-    unpack(4, "F", 0, False, True, S.fin)
+    TE.wait_ge(S.v2, 8)
+    unpack(0, "F", 0, S.fin)
     segs = []
     for q in peers + [l]:
         if segs and segs[-1][1] + segs[-1][2] == C0[q]:
@@ -183,9 +182,9 @@ def rank_program(g, core, T, topo):
         E.wait_ge(S.fin, t + 1)
         for x, j, n in segs:
             if t % 2 == 0:
-                V.tensor_copy(T.ysb[:, 4 * j + t:4 * (j + n):4], bank(4 + t, x, x + n)).then_inc(S.ycp, 1)
+                V.tensor_copy(T.ysb[:, 4 * j + t:4 * (j + n):4], bank(t, x, x + n)).then_inc(S.ycp, 1)
             else:
-                SC.activation(T.ysb[:, 4 * j + t:4 * (j + n):4], bank(4 + t, x, x + n),
+                SC.activation(T.ysb[:, 4 * j + t:4 * (j + n):4], bank(t, x, x + n),
                               ActivationFunctionType.Copy).then_inc(S.ycp, 1)
     SY.wait_ge(S.ycp, 4 * len(segs))
     SY.dma_start(T.y[:], T.ysb[:]).then_inc(S.sty, 16)

from concourse.bass import DstId, RemoteDMATransfer
from concourse.mybir import dt, AluOpType, ActivationFunctionType

NCOL = 128
W = [48, 32, 48]
C0 = [0, 48, 80]
WMAX = 48

CODE, U8, BF, F32 = "float8_e4m3fn_x4", "uint8", "bfloat16", "float32"
SCRATCH = {
    "ta": ("sbuf", [128, 2048], BF), "tb": ("sbuf", [128, 512], BF),
    "ones": ("sbuf", [128, 128], BF), "ident": ("sbuf", [128, 128], BF), "tz": ("sbuf", [128, 2048], BF),
    "tt": ("sbuf", [128, 512], BF), "st": ("sbuf", [128, 512], BF), "et": ("sbuf", [128, 512], BF),
    "tmp": ("sbuf", [128, 4 * WMAX], F32), "tmp2": ("sbuf", [128, 4 * WMAX], F32), "es": ("sbuf", [128, 4 * WMAX], F32),
    "ysb": ("sbuf", [128, 512], F32),
    "qa": ("sbuf", [128, 512], CODE), "qa_s": ("sbuf", [128, 512], U8),
    "qb": ("sbuf", [128, 128], CODE), "qb_s": ("sbuf", [128, 128], U8),
    "qz": ("sbuf", [128, 512], CODE), "qz_s": ("sbuf", [128, 512], U8),
    "L": ("sbuf", [128, 4 * WMAX + NCOL], CODE), "L_s": ("sbuf", [128, 4 * WMAX + NCOL], U8),
    "G": ("sbuf", [128, NCOL + WMAX], CODE), "G_s": ("sbuf", [128, NCOL + WMAX], U8),
    "F": ("sbuf", [128, 2 * NCOL], CODE), "F_s": ("sbuf", [128, 2 * NCOL], U8),
    "ps": ("psum", [128, 512 * 8], F32),
}
SEMAPHORES = ["ld_b", "ld_a0", "ld_a3", "c_one", "c_mem", "c_id", "c_z", "c_qz", "q_b", "q_a", "p_t",
              "cp_t", "q_t", "u1", "v1", "q_s", "u2", "v2", "u3", "v3", "q_e", "fin", "ycp", "sty",
              "arrA", "arrNm", "arrNp", "arrD", "arrE", "left"]


def rank_program(g, core, T, topo):
    if T.rank_of(core) is None:
        return
    S = T.sem
    hosts = sorted({topo.host(c) for c in T.cores})
    lanes = {h: [c for c in T.cores if topo.host(c) == h] for h in hosts}
    ring = [hosts[0]]
    while len(ring) < len(hosts):
        ring.append([x for x in hosts if x not in ring and topo.may_write(lanes[ring[-1]][0], lanes[x][0])][0])
    h = topo.host(core)
    l = lanes[h].index(core)
    pos = ring.index(h)
    nxt = lanes[ring[(pos + 1) % len(ring)]][l]
    prv = lanes[ring[(pos - 1) % len(ring)]][l]
    peers = [(l + 1) % 3, (l + 2) % 3]
    w, c0 = W[l], C0[l]
    q0 = 2 * w + 2 * WMAX

    def xoff(p, lane):
        order = [(p + 1) % 3, (p + 2) % 3, p]
        return sum(W[q] for q in order[:order.index(lane)])

    def bits(dsts):
        m = topo.mask(core, dsts[0])
        for d in dsts[1:]:
            m &= topo.mask(core, d)
        return [1 << i for i in range(16) if (m >> i) & 1]

    def did(d):
        rid, pid = topo.addr(d, core)
        return DstId(rid=rid, pnc=pid)

    def send(pairs, sem):
        eng = bits([p[0] for p in pairs])
        k = len(eng) // len(pairs)
        for plane in (False, True):
            tr = []
            for i, (d, sb, a, b, lb, c) in enumerate(pairs):
                if plane:
                    src, dst = T[sb + "_s"][:, a:b], T[lb + "_s"][:, c:c + b - a]
                else:
                    src, dst = T[sb][:, a:b].bitcast(dt.uint8), T[lb][:, c:c + b - a].bitcast(dt.uint8)
                tr.append(RemoteDMATransfer(dst_ids=[did(d)], dma_engine_mask=sum(eng[i * k:(i + 1) * k]),
                                            remote_sem=sem, src=src, dst=dst))
            g.remote_dma_fused(tr, local_sem=S.left)
        return 2 * k * len(pairs)

    V, SC, TE, SY = g.vector, g.scalar, g.tensor, g.sync
    bank = lambda i, a, b: T.ps[:, 512 * i + a:512 * i + b]

    SY.dma_start(T.tb[:], T.b[:]).then_inc(S.ld_b, 16)
    SC.dma_start(T.ta[:, 0:1536], T.a[:, 0:1536]).then_inc(S.ld_a0, 16)
    SY.dma_start(T.ta[:, 1536:2048], T.a[:, 1536:2048]).then_inc(S.ld_a3, 16)

    V.memset(T.ones[:], 1.0).then_inc(S.c_one, 1)
    V.memset(T.tz[:], 0.0).then_inc(S.c_mem, 1)
    g.wait_ge(S.c_one, 1)
    g.affine_select(T.ident[:], T.ones[:], [[-1, 128]], AluOpType.is_equal, 0.0, 0, 1).then_inc(S.c_id, 1)
    V.wait_ge(S.c_mem, 1)
    V.wait_ge(S.c_id, 1)
    for t in range(4):
        V.tensor_copy(T.tz[:, 512 * t + t:512 * t + 512:4], T.ident[:]).then_inc(S.c_z, 1)

    V.wait_ge(S.ld_b, 16)
    V.quantize_mx(T.qb[:], T.qb_s[:], T.tb[:]).then_inc(S.q_b, 1)
    TE.wait_ge(S.q_b, 1)
    V.wait_ge(S.ld_a0, 16)
    for t in range(4):
        cs = slice(128 * t, 128 * t + 128)
        if t == 3:
            V.wait_ge(S.ld_a3, 16)
        V.quantize_mx(T.qa[:, cs], T.qa_s[:, cs], T.ta[:, 512 * t:512 * t + 512]).then_inc(S.q_a, 1)
        TE.wait_ge(S.q_a, t + 1)
        TE.matmul_mx(bank(t, 0, 128), T.qa[:, cs], T.qa_s[:, cs], T.qb[:], T.qb_s[:], True, True).then_inc(S.p_t, 1)
        if t < 3:
            SC.wait_ge(S.p_t, t + 1)
            SC.activation(T.tt[:, t:512:4], bank(t, 0, 128), ActivationFunctionType.Copy).then_inc(S.cp_t, 1)
    V.wait_ge(S.p_t, 4)
    V.tensor_copy(T.tt[:, 3:512:4], bank(3, 0, 128)).then_inc(S.cp_t, 1)
    V.wait_ge(S.cp_t, 4)
    V.quantize_mx(T.L[:, q0:q0 + 128], T.L_s[:, q0:q0 + 128], T.tt[:]).then_inc(S.q_t, 1)
    V.wait_ge(S.c_z, 4)
    V.quantize_mx(T.qz[:], T.qz_s[:], T.tz[:]).then_inc(S.c_qz, 1)
    V.memset(T.st[:], 0.0).then_inc(S.c_mem, 1)
    V.memset(T.et[:], 0.0).then_inc(S.c_mem, 1)
    V.wait_ge(S.c_mem, 3)

    left = 0
    g.wait_ge(S.q_t, 1)
    left += send([(lanes[h][p], "L", q0 + C0[p], q0 + C0[p] + WMAX, "L",
                   2 * W[p] + WMAX * (0 if l == (p + 1) % 3 else 1)) for p in peers], S.arrA)

    def unpack(first_bank, buf, col, sem):
        for t in range(4):
            TE.matmul_mx(bank(first_bank + t, 0, 128), T.qz[:, 128 * t:128 * t + 128], T.qz_s[:, 128 * t:128 * t + 128],
                         T[buf][:, col:col + 128], T[buf + "_s"][:, col:col + 128], True, True).then_inc(sem, 1)

    def add3(first_bank, o1, o2, own, ostart, tmp, outs, usem, vsem):
        for t in range(4):
            V.wait_ge(usem, t + 1)
            V.tensor_tensor(tmp[:, WMAX * t:WMAX * t + w], bank(first_bank + t, o1, o1 + w),
                            own[:, 4 * ostart + t:4 * (ostart + w):4], AluOpType.add).then_inc(vsem, 1)
            V.wait_ge(vsem, 2 * t + 1)
            V.tensor_tensor(outs[t], bank(first_bank + t, o2, o2 + w), tmp[:, WMAX * t:WMAX * t + w],
                            AluOpType.add).then_inc(vsem, 1)
        V.wait_ge(vsem, 8)

    TE.wait_ge(S.c_qz, 1)
    TE.wait_ge(S.q_t, 1)
    TE.wait_ge(S.arrA, 16)
    unpack(4, "L", 2 * w, S.u1)
    add3(4, 0, WMAX, T.tt, c0, T.tmp, [T.st[:, t:4 * w:4] for t in range(4)], S.u1, S.v1)
    V.quantize_mx(T.G[:, 0:128], T.G_s[:, 0:128], T.st[:]).then_inc(S.q_s, 1)

    g.wait_ge(S.q_s, 1)
    left += send([(prv, "G", 0, w, "L", w)], S.arrNp)
    left += send([(nxt, "G", 0, w, "L", 0)], S.arrNm)
    g.wait_ge(S.arrNp, 16)
    left += send([(prv, "L", w, 2 * w, "G", NCOL)], S.arrD)

    TE.wait_ge(S.arrNp, 16)
    TE.wait_ge(S.arrNm, 16)
    TE.wait_ge(S.cp_t, 4)
    unpack(0, "L", 0, S.u2)
    add3(0, 0, w, T.st, 0, T.tmp2, [T.es[:, WMAX * t:WMAX * t + w] for t in range(4)], S.u2, S.v2)

    TE.wait_ge(S.arrD, 16)
    TE.wait_ge(S.q_s, 1)
    TE.wait_ge(S.v1, 8)
    unpack(4, "G", w, S.u3)
    for t in range(4):
        V.wait_ge(S.u3, t + 1)
        V.tensor_tensor(T.et[:, t:4 * w:4], bank(4 + t, NCOL - w, NCOL), T.es[:, WMAX * t:WMAX * t + w],
                        AluOpType.add).then_inc(S.v3, 1)
    V.wait_ge(S.v3, 4)
    e0 = xoff(l, l)
    V.quantize_mx(T.F[:, e0:e0 + 128], T.F_s[:, e0:e0 + 128], T.et[:]).then_inc(S.q_e, 1)

    g.wait_ge(S.q_e, 1)
    left += send([(lanes[h][p], "F", e0, e0 + w, "F", xoff(p, l)) for p in peers], S.arrE)

    TE.wait_ge(S.arrE, 16)
    TE.wait_ge(S.q_e, 1)
    TE.wait_ge(S.v2, 8)
    unpack(0, "F", 0, S.fin)
    segs = []
    for q in peers + [l]:
        if segs and segs[-1][1] + segs[-1][2] == C0[q]:
            segs[-1] = (segs[-1][0], segs[-1][1], segs[-1][2] + W[q])
        else:
            segs.append((xoff(l, q), C0[q], W[q]))
    for t in range(4):
        E = V if t % 2 == 0 else SC
        E.wait_ge(S.fin, t + 1)
        for x, j, n in segs:
            if t % 2 == 0:
                V.tensor_copy(T.ysb[:, 4 * j + t:4 * (j + n):4], bank(t, x, x + n)).then_inc(S.ycp, 1)
            else:
                SC.activation(T.ysb[:, 4 * j + t:4 * (j + n):4], bank(t, x, x + n),
                              ActivationFunctionType.Copy).then_inc(S.ycp, 1)
    SY.wait_ge(S.ycp, 4 * len(segs))
    SY.dma_start(T.y[:], T.ysb[:]).then_inc(S.sty, 16)
    SY.wait_ge(S.sty, 16)
    g.wait_ge(S.left, left)
